import numpy as np
import ml_dtypes


def mxq(x, axis, fmt="e4m3"):
    dtype, down = {"e4m3": (ml_dtypes.float8_e4m3fn, 7), "e5m2": (ml_dtypes.float8_e5m2, 14)}[fmt]
    v = np.moveaxis(np.asarray(x, np.float32).astype(ml_dtypes.bfloat16).astype(np.float64), axis, -1)
    blocks = v.reshape(v.shape[:-1] + (-1, 32))
    amax = np.abs(blocks).max(-1, keepdims=True)
    byte = np.maximum(np.where(amax > 0, np.frexp(amax)[1] - 1 + 127, 0) - down, 1)
    scale = np.exp2(byte - 127.0)
    codes = (blocks / scale).astype(np.float32).astype(dtype).astype(np.float64)
    return np.moveaxis((codes * scale).reshape(v.shape), -1, axis)


WIDE = False


def mx_kscale(k):
    if not WIDE:
        return np.ones(k)
    levels = np.array([10, -10, 5, -5, 0])
    if k % 512:
        return np.exp2(np.random.permutation(np.resize(levels, k // 32))).repeat(32)
    a = np.empty((k // 512, 16))
    for p in range(k // 512):
        a[p, :8] = np.random.permutation(np.resize(levels, 8))
        for g in range(8):
            far = levels[np.abs(levels - a[p, g]) >= 10]
            a[p, g + 8] = far[np.random.randint(len(far))]
    return np.exp2(a.ravel()).repeat(32)


BF16 = ml_dtypes.bfloat16


def bf(x):
    return np.asarray(x, np.float32).astype(BF16)


def f64(x):
    return np.asarray(x).astype(np.float64)


E2M1 = np.array([0.0, 0.5, 1.0, 1.5, 2.0, 3.0, 4.0, 6.0, -0.0, -0.5, -1.0, -1.5, -2.0, -3.0, -4.0, -6.0])


def pack_weight(w, fmt):
    k, n = w.shape
    w = f64(bf(w)).reshape(k // 32, 32, n)
    amax = np.abs(w).max(1)
    if fmt == "e4m3":
        byte = np.frexp(amax)[1] - 1 + 127 - 7
    else:
        mant, ex = np.frexp(amax / 6.0)
        byte = np.where(mant > 0.5, ex, ex - 1) + 127
    byte = np.clip(np.where(amax > 0, byte, 1), 1, 254)
    scaled = (w * np.exp2(127.0 - byte)[:, None, :]).reshape(k, n).astype(np.float32)
    by_word = np.ascontiguousarray(scaled.reshape(k // 512, 128, 4, n).transpose(0, 1, 3, 2))
    if fmt == "e4m3":
        words = by_word.astype(ml_dtypes.float8_e4m3fn).view(np.uint8)
    else:
        c = by_word.astype(ml_dtypes.float4_e2m1fn).view(np.uint8) & 0xF
        words = c[..., 0::2] | (c[..., 1::2] << 4)
    return np.ascontiguousarray(words), np.ascontiguousarray(byte.astype(np.uint8).reshape(k // 512, 16, n))


def unpack_weight(words, scales, fmt):
    g, p, n, _ = words.shape
    if fmt == "e4m3":
        vals = np.ascontiguousarray(words).view(ml_dtypes.float8_e4m3fn).astype(np.float64)
    else:
        nib = np.empty((g, p, n, 4), np.uint8)
        nib[..., 0::2] = words & 0xF
        nib[..., 1::2] = words >> 4
        vals = E2M1[nib]
    vals = vals * np.repeat(np.exp2(scales.astype(np.float64) - 127.0), 8, axis=1)[..., None]
    return vals.transpose(0, 1, 3, 2).reshape(g * 512, n)
def pack4(w):
    words, scales = pack_weight(w, "e2m1")
    return words.reshape(words.shape[0], 128, -1), scales


def unpack4(words, scales):
    return unpack_weight(words.reshape(words.shape[0], 128, -1, 2), scales, "e2m1")


E4M3FN = np.array([(-1.0 if i & 128 else 1.0) * ((1.0 + (i & 7) / 8.0) * 2.0 ** (((i >> 3) & 15) - 7) if i & 120 else (i & 7) * 2.0 ** -9) for i in range(256)])


def e4m3fn_bytes(y):
    return np.clip(np.asarray(y, np.float64), -448.0, 448.0).astype(np.float32).astype(ml_dtypes.float8_e4m3fn).view(np.uint8)


def e4m3fn_values(b):
    return E4M3FN[b]


B, S, D, M, N, C = 2, 1024, 512, 512, 512, 2


def cauchy_parts(om, nu, b):
    de = om[:, None] - nu[None, :]
    w = b[None, :] / (0.25 + de * de)
    gr = 0.5 * w
    gi = -de * w
    return gr, gi


def draw0():
    s, t, r = mx_kscale(S), mx_kscale(M), mx_kscale(N)
    x = bf(np.random.standard_normal((B, S, D)) / s[None, :, None])
    p = np.random.standard_normal((M, S)) / np.sqrt(S) * s[None, :] * t[:, None]
    p_words, p_scales = pack4(p.T)
    om = bf(np.random.uniform(-4.0, 4.0, M))
    nu = bf(np.random.uniform(-4.0, 4.0, N))
    b = bf(np.random.standard_normal(N) * r)
    c = np.random.standard_normal((N, D)) * 1.5 / np.sqrt(N) / r[:, None]
    c_words, c_scales = pack4(c)
    q = bf(np.random.standard_normal((C, S, M)) / np.sqrt(M) / t[None, None, :])
    return {"x": x,
            "p_words": p_words,
            "p_scales": p_scales,
            "om": om,
            "nu": nu,
            "b": b,
            "c_words": c_words,
            "c_scales": c_scales,
            "q": q}


def core(x, p_words, p_scales, om, nu, b, c_words, c_scales, q):
    gr, gi = cauchy_parts(f64(om), f64(nu), f64(b))
    gr, gi = gr, gi
    cq = unpack4(c_words, c_scales)
    kr = mxq(gr, 1, "e4m3") @ cq
    ki = mxq(gi, 1, "e4m3") @ cq
    u = unpack4(p_words, p_scales).T @ mxq(f64(x), 1, "e4m3")
    fr = kr[None, :, :] * u
    fi = ki[None, :, :] * u
    qq = mxq(f64(q), 2, "e4m3")
    return (qq[0] @ mxq(fr, 1, "e4m3")) - (qq[1] @ mxq(fi, 1, "e4m3"))


def setup_inputs():
    drawn = draw0()
    full = np.asarray(drawn['x']).astype(np.float64)
    scale = (np.abs(full).reshape(2, 8, 128, 4, 128).max(axis=(2, 4)) / 448.0).astype(np.float32)
    given = {}
    for key, value in drawn.items():
        if key == 'x':
            given['x_bytes'] = e4m3fn_bytes(full / np.repeat(np.repeat(scale.astype(np.float64), 128, axis=1), 128, axis=2))
            given['x_scale'] = scale
        else:
            given[key] = value
    return given


def reference(x_bytes, x_scale, p_words, p_scales, om, nu, b, c_words, c_scales, q):
    return core(e4m3fn_values(x_bytes) * np.repeat(np.repeat(x_scale.astype(np.float64), 128, axis=1), 128, axis=2), p_words, p_scales, om, nu, b, c_words, c_scales, q)

@@ -1,0 +1,334 @@
+from contextlib import ExitStack
+
+import concourse.mybir as mybir
+from concourse.masks import make_identity
+
+F32 = mybir.dt.float32
+BF16 = mybir.dt.bfloat16
+U32 = mybir.dt.uint32
+I32 = mybir.dt.int32
+U8 = mybir.dt.uint8
+FP8 = mybir.dt.float8_e4m3fn
+E4M3 = mybir.dt.float8_e4m3fn_x4
+E2M1 = mybir.dt.float4_e2m1fn_x4
+ALU = mybir.AluOpType
+ACT = mybir.ActivationFunctionType
+
+B, S, D, M, N = 2, 1024, 512, 512, 512
+P = 128
+FLOPS = 2 * (2 * M * N * D + B * M * S * D + 2 * B * S * M * D)
+
+ORDER = """
+de.1 de.3 xi.0 sq.1 de.0 sq.3 de.2 sq.0 xi.1 ars.1 sq.2 xw.0.2.V
+pw.0 xi.3 ars.3 ars.2 pw.1 xi.2 ars.0 xw.1.3.S tr.1.1 xw.3.2.V ps xw.0.3.S
+tr.0.1 w.1 xw.2.0.S tr.0.0 w.2 xw.3.3.S tr.2.0 w.3 qc.1.1 w.0 xw.0.0.S tr.2.1
+xw.1.2.V xw.3.1.S gi.2 qc.0.1 gi.1 qc.2.1 gr tr.3.0 xw.2.3.S xw.0.1.S gi.0 xw.1.1.S
+gi.3 xw.2.2.S gq.0 xw.1.0.S gq.1 qc.0.0 k.2.0 k.3.0 xq.0 xw.2.1.S tr.1.0 kc.2.0
+qq.0 tr.3.1 qc.1.0 xq.1 k.3.1 k.0.1 xw.3.0.S xq.2 k.2.1 qc.2.0 u.0.2 qq.1
+kc.2.1 k.1.0 xq.3 kc.3.0 u.0.3 qq.2 qc.3.0 u.1.1 tt.0.2 kc.3.1 qc.3.1 k.1.1
+u.1.0 tt.0.3 kc.1.0 u.0.1 kc.0.1 qq.3 kc.1.1 k.0.0 u.0.0 fq.0.1 kc.0.0 tt.0.1
+sy.0.1.3 sy.0.1.0 tt.0.0 oc.0.1.3.S sy.0.1.1 oc.0.1.0.S u.1.3 tt.1.1 oc.0.1.1.S sy.0.1.2 u.1.2 fq.0.0
+oc.0.1.2.S tt.1.0 sy.0.0.3 sy.0.0.2 oc.0.0.3.S fq.1.0 sy.0.0.0 oc.0.0.2.S sy.0.0.1 tt.1.2 oc.0.0.0.S sy.1.0.3
+oc.0.0.1.S sy.1.0.0 oc.1.0.3.S fq.1.1.2 sy.1.0.2 tt.1.3 oc.1.0.0.S sy.1.0.1 oc.1.0.2.S sy.1.1.2.0 oc.1.0.1.S fq.1.1.3
+sy.1.1.2.1 oc.1.1.2.0.S sy.1.1.3.0 oc.1.1.2.1.V sy.1.1.3.1 oc.1.1.3.0.V oc.1.1.3.1.V
+"""
+
+
+def tile_cauchytransferfunctionfilter_d2p_kernel(
+    tc, x_bytes, x_scale, p_words, p_scales, om, nu, b, c_words, c_scales, q, out
+):
+    nc = tc.nc
+    with ExitStack() as ctx:
+        keep = ctx.enter_context(tc.tile_pool(name="keep", bufs=1))
+        psum = ctx.enter_context(tc.psum_pool(name="psum", bufs=8))
+        ctx.enter_context(tc.manual_schedule())
+
+        def bank(name):
+            return psum.tile([P, 512], F32, tag="bank", name=name)
+
+        def sb(name, shape, dt):
+            return keep.tile(shape, dt, name=name, align_bytes=64)
+
+        right = sb("right", [P, 512], BF16)
+        left = sb("left", [P, 512], BF16)
+        warm = sb("warm", [P, 8], F32)
+        warm2 = sb("warm2", [P, 8], F32)
+        c_s = sb("c_s", [P, 512], U8)
+        p_s_raw = sb("p_s_raw", [P, 2, 512], U8)
+        ident = sb("ident", [P, P], F32)
+        x_raw = [sb("x_raw%d" % a, [P, 4, D], U8) for a in range(4)]
+        x_all = sb("x_all", [P, 64], F32)
+        x_s = sb("x_s", [P, 16], F32)
+        b_col = sb("b_col", [P, 4], BF16)
+        c_w = sb("c_w", [P, 1024], U8)
+        p_w_raw = sb("p_w_raw", [P, 2, 1024], U8)
+        q_raw = sb("q_raw", [P, 2, 8, M], BF16)
+        x_view = x_bytes.rearrange("i (g p t) d -> (i g) p t d", p=P, t=4)
+
+        nc.vector.memset(right[:], 0.0)
+        nc.gpsimd.memset(left[:], 1.0)
+        nc.vector.memset(right[32:33, :], -1.0)
+        nc.vector.memset(warm[:], 1.0)
+        nc.vector.memset(c_s[:].bitcast(I32), 0)
+        nc.gpsimd.memset(p_s_raw[:].rearrange("p g n -> p (g n)").bitcast(I32), 0)
+
+        nc.sync.dma_start(out=x_raw[0][:], in_=x_view[0])
+        nc.sync.dma_start(out=right[0:1, :], in_=om.rearrange("(o m) -> o m", o=1))
+        nc.sync.dma_start(out=left[32:33, :], in_=nu.rearrange("(o n) -> o n", o=1))
+        nc.scalar.dma_start(out=x_all[:], in_=x_scale.rearrange("i s j -> (i s j)").partition_broadcast(P))
+        nc.scalar.dma_start(out=b_col[:], in_=b.rearrange("(p t) -> p t", t=4))
+        nc.scalar.activation(out=warm2[:], in_=warm[:], func=ACT.Abs_reciprocal_sqrt, bias=0.25)
+        for quad in range(4):
+            nc.gpsimd.dma_start(
+                out=c_s[32 * quad : 32 * quad + 4, :].bitcast(I32),
+                in_=c_scales[0, 4 * quad : 4 * quad + 4, :].bitcast(I32),
+            )
+        for a in range(1, 4):
+            nc.sync.dma_start(out=x_raw[a][:], in_=x_view[a])
+        nc.sync.dma_start(out=p_w_raw[:].bitcast(I32), in_=p_words.rearrange("g p n -> p g n").bitcast(I32))
+        for quad in range(4):
+            nc.sync.dma_start(
+                out=p_s_raw[32 * quad : 32 * quad + 4, :, :].bitcast(I32),
+                in_=p_scales[:, 4 * quad : 4 * quad + 4, :].rearrange("g r n -> r g n").bitcast(I32),
+            )
+        nc.sync.dma_start(out=c_w[:].bitcast(I32), in_=c_words[0].bitcast(I32))
+        for h in range(2):
+            for c in range(2):
+                nc.sync.dma_start(
+                    out=q_raw[:, c, 4 * h : 4 * h + 4, :],
+                    in_=q[c].rearrange("(p j) m -> p j m", j=8)[:, 4 * h : 4 * h + 4, :],
+                )
+        for quad in range(4):
+            rows = slice(32 * quad, 32 * quad + 32)
+            nc.gpsimd.tensor_copy(
+                out=x_s[rows, :].rearrange("p (a j) -> p a j", j=4),
+                in_=x_all[rows, :].rearrange("p (a s j) -> p a s j", s=4, j=4)[:, :, quad, :],
+            )
+        make_identity(nc, ident[:])
+
+        sq = sb("sq", [P, 4, 512], F32)
+        root = sb("root", [P, 4, 512], F32)
+        w = sb("w", [P, 4, 512], F32)
+        g_bf = [sb("g_bf%d" % c, [P, 512, 4], BF16) for c in range(2)]
+        g_c = [sb("g_c%d" % c, [P, 512], U32) for c in range(2)]
+        g_cs = [sb("g_cs%d" % c, [P, 512], U8) for c in range(2)]
+        k = sb("k", [P, 4, 2, 128, 4], F32)
+        p_w = sb("p_w", [P, 2, 1024], U8)
+        p_s = sb("p_s", [P, 2, 512], U8)
+        x_il = [sb("x_il%d" % a, [P, D, 4], U8) for a in range(4)]
+        x_bf = [sb("x_bf%d" % a, [P, D * 4], BF16) for a in range(4)]
+        x_c = [sb("x_c%d" % i, [P, 2, D], U32) for i in range(2)]
+        x_cs = [sb("x_cs%d" % i, [P, 2, D], U8) for i in range(2)]
+        q_bf = [sb("q_bf%d" % n, [P, 4, 128, 4], BF16) for n in range(4)]
+        q_c = [sb("q_c%d" % n, [P, 512], U32) for n in range(4)]
+        q_cs = [sb("q_cs%d" % n, [P, 512], U8) for n in range(4)]
+        q_words = q_raw[:].rearrange("p c j m -> p (c j m)").bitcast(F32)
+        f_bf = [[sb("f_bf%d%d" % (i, h), [P, 2, 2, 128, 4], BF16) for h in range(2)] for i in range(2)]
+        f_c = [[sb("f_c%d%d" % (i, h), [P, 2, 2, 128], U32) for h in range(2)] for i in range(2)]
+        f_cs = [[sb("f_cs%d%d" % (i, h), [P, 2, 2, 128], U8) for h in range(2)] for i in range(2)]
+        o = [[sb("o%d%d" % (i, h), [P, 8, 256], F32) for h in range(2)] for i in range(2)]
+        banks = {}
+
+        def cols(n, width=128):
+            return slice(width * n, width * n + width)
+
+        def de(t):
+            d = banks["de", t] = bank("de%d" % t)
+            for tn in range(4):
+                nc.tensor.matmul(d[:, cols(tn)], lhsT=left[:, tn::4], rhs=right[:, t::4], start=True, stop=True)
+
+        def do_sq(t):
+            nc.scalar.activation(
+                out=sq[:, :, cols(t)], in_=banks["de", t][:].rearrange("p (t m) -> p t m", t=4), func=ACT.Square
+            )
+
+        def ars(t):
+            nc.scalar.activation(out=root[:, :, cols(t)], in_=sq[:, :, cols(t)], func=ACT.Abs_reciprocal_sqrt, bias=0.25)
+
+        def do_w(t):
+            nc.vector.scalar_tensor_tensor(
+                out=w[:, t, :], in0=root[:, t, :], scalar=b_col[:, t : t + 1], in1=root[:, t, :],
+                op0=ALU.mult, op1=ALU.mult,
+            )
+
+        def gr():
+            nc.vector.tensor_scalar(
+                out=g_bf[0][:], in0=w[:].rearrange("p t m -> p m t"), scalar1=0.5, scalar2=None, op0=ALU.mult
+            )
+
+        def gi(t):
+            nc.vector.tensor_tensor(
+                out=g_bf[1][:, cols(t), :],
+                in0=banks["de", t][:].rearrange("p (t m) -> p m t", t=4),
+                in1=w[:, :, cols(t)].rearrange("p t m -> p m t"),
+                op=ALU.mult,
+            )
+
+        def gq(c):
+            nc.vector.quantize_mx(
+                out=g_c[c][:].bitcast(E4M3), scales=g_cs[c][:], in_=g_bf[c][:].rearrange("p m t -> p (m t)")
+            )
+
+        def do_k(blk, c):
+            kb = banks["k", blk, c] = bank("k%d%d" % (blk, c))
+            for t in range(4):
+                nc.tensor.matmul_mx(
+                    out=kb[:, cols(t)],
+                    lhsT=g_c[c][:, cols(t)].bitcast(E4M3),
+                    lhsT_scale=g_cs[c][:, cols(t)],
+                    rhs=c_w[:, cols(blk, 256)].bitcast(E2M1),
+                    rhs_scale=c_s[:, cols(blk)],
+                    start=True,
+                    stop=True,
+                )
+
+        def kc(blk, c):
+            nc.scalar.copy(out=k[:, blk, c, :, :], in_=banks["k", blk, c][:].rearrange("p (t d) -> p d t", t=4))
+
+        def pw(g):
+            nc.gpsimd.tensor_copy(
+                out=p_w[:, g, :].rearrange("p (t n e) -> p t n e", t=4, e=2),
+                in_=p_w_raw[:, g, :].rearrange("p (n t e) -> p t n e", t=4, e=2),
+            )
+
+        def ps():
+            nc.gpsimd.tensor_copy(
+                out=p_s[:].rearrange("p g (t n) -> p g t n", t=4),
+                in_=p_s_raw[:].rearrange("p g (n t) -> p g t n", t=4),
+            )
+
+        def xi(a):
+            nc.vector.tensor_copy(out=x_il[a][:], in_=x_raw[a][:].rearrange("p t d -> p d t"))
+
+        def xw(a, j, eng="S"):
+            src = x_il[a][:].rearrange("p d t -> p (d t)")[:, cols(j, 512)].bitcast(FP8)
+            dst = x_bf[a][:, cols(j, 512)]
+            scale = x_s[:, 4 * a + j : 4 * a + j + 1]
+            if eng == "V":
+                nc.vector.tensor_scalar(out=dst, in0=src, scalar1=scale, scalar2=None, op0=ALU.mult)
+            else:
+                nc.scalar.activation(out=dst, in_=src, func=ACT.Copy, scale=scale)
+
+        def xq(a):
+            i, g = a // 2, a % 2
+            nc.vector.quantize_mx(out=x_c[i][:, g, :].bitcast(E4M3), scales=x_cs[i][:, g, :], in_=x_bf[a][:])
+
+        def tr(n, pair):
+            h, c = n // 2, n % 2
+            tb = banks["tr", n, pair] = bank("tr%d%d" % (n, pair))
+            for s in range(2):
+                base = (c * 8 + 4 * h + 2 * pair + s) * 256
+                for u in range(2):
+                    nc.tensor.transpose(tb[:, cols(2 * s + u)], q_words[:, base + u : base + 256 : 2], ident[:])
+
+        def qc(n, pair):
+            nc.scalar.copy(
+                out=q_bf[n][:, 2 * pair : 2 * pair + 2, :, :]
+                .rearrange("p s r e -> p (s r e)")
+                .bitcast(F32)
+                .rearrange("p (s r u) -> p s r u", s=2, u=2),
+                in_=banks["tr", n, pair][:].rearrange("p (s u r) -> p s r u", s=2, u=2),
+            )
+
+        def qq(n):
+            nc.vector.quantize_mx(
+                out=q_c[n][:].bitcast(E4M3), scales=q_cs[n][:], in_=q_bf[n][:].rearrange("p s r e -> p (s r e)")
+            )
+
+        def do_u(i, blk):
+            ub = banks["u", i, blk] = bank("u%d%d" % (i, blk))
+            for t in range(4):
+                for g in range(2):
+                    nc.tensor.matmul_mx(
+                        out=ub[:, cols(t)],
+                        lhsT=p_w[:, g, cols(t, 256)].bitcast(E2M1),
+                        lhsT_scale=p_s[:, g, cols(t)],
+                        rhs=x_c[i][:, g, cols(blk)].bitcast(E4M3),
+                        rhs_scale=x_cs[i][:, g, cols(blk)],
+                        start=(g == 0),
+                        stop=(g == 1),
+                    )
+
+
+        def tt(i, blk):
+            h = blk // 2
+            dst = f_bf[i][h][:, blk % 2] if (i, h) == (1, 1) else f_bf[i][h][:, :, blk % 2]
+            nc.vector.tensor_tensor(
+                out=dst,
+                in0=banks["u", i, blk][:].rearrange("p (t d) -> p d t", t=4).unsqueeze(1).to_broadcast([P, 2, 128, 4]),
+                in1=k[:, blk],
+                op=ALU.mult,
+            )
+
+        def fq(i, h, blk=None):
+            if blk is None:
+                nc.vector.quantize_mx(
+                    out=f_c[i][h][:].rearrange("p a b d -> p (a b d)").bitcast(E4M3),
+                    scales=f_cs[i][h][:].rearrange("p a b d -> p (a b d)"),
+                    in_=f_bf[i][h][:].rearrange("p a b d t -> p (a b d t)"),
+                )
+            else:
+                nc.vector.quantize_mx(
+                    out=f_c[i][h][:, blk % 2].rearrange("p c d -> p (c d)").bitcast(E4M3),
+                    scales=f_cs[i][h][:, blk % 2].rearrange("p c d -> p (c d)"),
+                    in_=f_bf[i][h][:, blk % 2].rearrange("p c d t -> p (c d t)"),
+                )
+
+        def q_at(j, c):
+            n = 2 * (j // 4) + c
+            return q_c[n][:, cols(j % 4)].bitcast(E4M3), q_cs[n][:, cols(j % 4)]
+
+        def sy(i, h, m, part=None):
+            if part is None:
+                ob = banks["sy", i, h, m] = bank("sy%d%d%d" % (i, h, m))
+                tiles, width = (2 * m, 2 * m + 1), 256
+            else:
+                blk, m = m, part
+                ob = banks["sy", i, h, blk, m] = bank("sy%d%d%d%d" % (i, h, blk, m))
+                tiles, width = (4 * m, 4 * m + 1, 4 * m + 2, 4 * m + 3), 128
+            for s in range(len(tiles)):
+                for c in range(2):
+                    codes, scales = q_at(tiles[s], c)
+                    if part is None:
+                        fc = f_c[i][h][:, c].rearrange("p b d -> p (b d)")
+                        fs = f_cs[i][h][:, c].rearrange("p b d -> p (b d)")
+                    else:
+                        fc = f_c[i][h][:, blk % 2, c]
+                        fs = f_cs[i][h][:, blk % 2, c]
+                    nc.tensor.matmul_mx(
+                        out=ob[:, cols(s, width)],
+                        lhsT=codes,
+                        lhsT_scale=scales,
+                        rhs=fc.bitcast(E4M3),
+                        rhs_scale=fs,
+                        start=(c == 0),
+                        stop=(c == 1),
+                    )
+
+        def oc(i, h, m, part=None, eng="S"):
+            if part is None:
+                src = banks["sy", i, h, m][:].rearrange("p (j d) -> p j d", j=2)
+                js, ds, do = slice(2 * m, 2 * m + 2), slice(256 * h, 256 * h + 256), slice(0, 256)
+            else:
+                blk, m = m, part
+                src = banks["sy", i, h, blk, m][:].rearrange("p (j d) -> p j d", j=4)
+                js, ds, do = slice(4 * m, 4 * m + 4), cols(blk), cols(blk % 2)
+            dst = o[i][h][:, js, do]
+            if eng == "V":
+                nc.vector.tensor_copy(out=dst, in_=src)
+            else:
+                nc.scalar.copy(out=dst, in_=src)
+            nc.sync.dma_start(out=out[i].rearrange("(p j) d -> p j d", j=8)[:, js, ds], in_=dst)
+
+        table = {
+            "de": de, "sq": do_sq, "ars": ars, "w": do_w, "gr": gr, "gi": gi, "gq": gq, "k": do_k, "kc": kc,
+            "pw": pw, "ps": ps, "xi": xi, "xw": xw, "xq": xq, "tr": tr, "qc": qc, "qq": qq, "u": do_u,
+            "tt": tt, "fq": fq, "sy": sy, "oc": oc,
+        }
+        for step in ORDER.split():
+            parts = step.split(".")
+            args = [int(z) for z in parts[1:] if z not in ("S", "V")]
+            if parts[0] in ("xw", "oc"):
+                table[parts[0]](*args, eng=parts[-1])
+            else:
+                table[parts[0]](*args)

@@ -19,18 +19,18 @@ P = 128
 FLOPS = 2 * (2 * M * N * D + B * M * S * D + 2 * B * S * M * D)
 
 ORDER = """
-de.1 de.3 xi.0 sq.1 de.0 sq.3 de.2 sq.0 xi.1 ars.1 sq.2 xw.0.2.V
-pw.0 xi.3 ars.3 ars.2 pw.1 xi.2 ars.0 xw.1.3.S tr.1.1 xw.3.2.V ps xw.0.3.S
-tr.0.1 w.1 xw.2.0.S tr.0.0 w.2 xw.3.3.S tr.2.0 w.3 qc.1.1 w.0 xw.0.0.S tr.2.1
-xw.1.2.V xw.3.1.S gi.2 qc.0.1 gi.1 qc.2.1 gr tr.3.0 xw.2.3.S xw.0.1.S gi.0 xw.1.1.S
-gi.3 xw.2.2.S gq.0 xw.1.0.S gq.1 qc.0.0 k.2.0 k.3.0 xq.0 xw.2.1.S tr.1.0 kc.2.0
-qq.0 tr.3.1 qc.1.0 xq.1 k.3.1 k.0.1 xw.3.0.S xq.2 k.2.1 qc.2.0 u.0.2 qq.1
-kc.2.1 k.1.0 xq.3 kc.3.0 u.0.3 qq.2 qc.3.0 u.1.1 tt.0.2 kc.3.1 qc.3.1 k.1.1
-u.1.0 tt.0.3 kc.1.0 u.0.1 kc.0.1 qq.3 kc.1.1 k.0.0 u.0.0 fq.0.1 kc.0.0 tt.0.1
-sy.0.1.3 sy.0.1.0 tt.0.0 oc.0.1.3.S sy.0.1.1 oc.0.1.0.S u.1.3 tt.1.1 oc.0.1.1.S sy.0.1.2 u.1.2 fq.0.0
-oc.0.1.2.S tt.1.0 sy.0.0.3 sy.0.0.2 oc.0.0.3.S fq.1.0 sy.0.0.0 oc.0.0.2.S sy.0.0.1 tt.1.2 oc.0.0.0.S sy.1.0.3
-oc.0.0.1.S sy.1.0.0 oc.1.0.3.S fq.1.1.2 sy.1.0.2 tt.1.3 oc.1.0.0.S sy.1.0.1 oc.1.0.2.S sy.1.1.2.0 oc.1.0.1.S fq.1.1.3
-sy.1.1.2.1 oc.1.1.2.0.S sy.1.1.3.0 oc.1.1.2.1.V sy.1.1.3.1 oc.1.1.3.0.V oc.1.1.3.1.V
+de.1 de.3 xi.0 sq.1 de.2 sq.3 de.0 xi.2 sq.2 xw.0.3.S pw.1 sq.0
+ars.1 xi.3 ars.0 ars.2 tr.0 xi.1 ars.3 xw.2.1.S tr.1 w.2 xw.3.2.S xw.3.1.V
+xw.2.3.S w.1 xw.0.1.S w.0 xw.2.2.S w.3 qc.1.0 pw.0 qc.1.1 gi.1 xw.1.1.S tr.3
+ps xw.1.2.S gr xw.0.2.S xw.1.0.S gi.2 xw.1.3.S xw.2.0.S gi.0 tr.2 xw.3.0.S gi.3
+xw.0.0.S gq.0 xw.3.3.S gq.1 k.3.0 qc.3.0 xq.0 qc.3.1 k.3.1 xq.1 k.2.1 qc.0.0
+qq.1 k.2.0 kc.2.1 u.0.2 xq.3 qc.0.1 xq.2 u.0.3 kc.3.0 qq.0 kc.3.1 k.0.1
+k.1.0 qq.3 kc.2.0 u.1.1 qc.2.1 tt.0.3 k.0.0 kc.1.0 u.1.3 tt.0.2 kc.0.0 u.0.0
+kc.0.1 tt.1.3 qc.2.0 u.1.2 k.1.1 fq.0.1 u.0.1 kc.1.1 fq.1.1.3 qq.2 sy.0.1.0 sy.1.1.3.0
+tt.0.1 oc.0.1.0.S sy.0.1.1 oc.1.1.3.0.S tt.0.0 sy.0.1.3 sy.1.1.3.1 oc.0.1.3.S tt.1.2 sy.0.1.2 oc.1.1.3.1.S u.1.0
+fq.0.0 oc.0.1.2.S fq.1.1.2 oc.0.1.1.S tt.1.0 sy.0.0.2 sy.0.0.3 oc.0.0.2.S tt.1.1 sy.1.1.2.0 oc.0.0.3.S sy.1.1.2.1
+oc.1.1.2.0.S sy.0.0.1 fq.1.0 oc.1.1.2.1.S sy.0.0.0 oc.0.0.1.V sy.1.0.3 oc.0.0.0.S sy.1.0.1 oc.1.0.3.V sy.1.0.2 oc.1.0.1.V
+sy.1.0.0 oc.1.0.2.V oc.1.0.0.S
 """
 
 
@@ -79,7 +79,7 @@ def tile_cauchytransferfunctionfilter_d2p_kernel(
         nc.scalar.dma_start(out=b_col[:], in_=b.rearrange("(p t) -> p t", t=4))
         nc.scalar.activation(out=warm2[:], in_=warm[:], func=ACT.Abs_reciprocal_sqrt, bias=0.25)
         for quad in range(4):
-            nc.gpsimd.dma_start(
+            nc.scalar.dma_start(
                 out=c_s[32 * quad : 32 * quad + 4, :].bitcast(I32),
                 in_=c_scales[0, 4 * quad : 4 * quad + 4, :].bitcast(I32),
             )
@@ -186,13 +186,13 @@ def tile_cauchytransferfunctionfilter_d2p_kernel(
             nc.scalar.copy(out=k[:, blk, c, :, :], in_=banks["k", blk, c][:].rearrange("p (t d) -> p d t", t=4))
 
         def pw(g):
-            nc.gpsimd.tensor_copy(
+            nc.vector.tensor_copy(
                 out=p_w[:, g, :].rearrange("p (t n e) -> p t n e", t=4, e=2),
                 in_=p_w_raw[:, g, :].rearrange("p (n t e) -> p t n e", t=4, e=2),
             )
 
         def ps():
-            nc.gpsimd.tensor_copy(
+            nc.vector.tensor_copy(
                 out=p_s[:].rearrange("p g (t n) -> p g t n", t=4),
                 in_=p_s_raw[:].rearrange("p g (n t) -> p g t n", t=4),
             )
@@ -213,13 +213,14 @@ def tile_cauchytransferfunctionfilter_d2p_kernel(
             i, g = a // 2, a % 2
             nc.vector.quantize_mx(out=x_c[i][:, g, :].bitcast(E4M3), scales=x_cs[i][:, g, :], in_=x_bf[a][:])
 
-        def tr(n, pair):
+        def tr(n):
             h, c = n // 2, n % 2
-            tb = banks["tr", n, pair] = bank("tr%d%d" % (n, pair))
-            for s in range(2):
-                base = (c * 8 + 4 * h + 2 * pair + s) * 256
-                for u in range(2):
-                    nc.tensor.transpose(tb[:, cols(2 * s + u)], q_words[:, base + u : base + 256 : 2], ident[:])
+            for pair in range(2):
+                tb = banks["tr", n, pair] = bank("tr%d%d" % (n, pair))
+                for s in range(2):
+                    base = (c * 8 + 4 * h + 2 * pair + s) * 256
+                    for u in range(2):
+                        nc.tensor.transpose(tb[:, cols(2 * s + u)], q_words[:, base + u : base + 256 : 2], ident[:])
 
         def qc(n, pair):
             nc.scalar.copy(
@@ -327,7 +328,7 @@ def tile_cauchytransferfunctionfilter_d2p_kernel(
         }
         for step in ORDER.split():
             parts = step.split(".")
-            args = [int(z) for z in parts[1:] if z not in ("S", "V")]
+            args = [int(z) for z in parts[1:] if z not in ("S", "V", "G")]
             if parts[0] in ("xw", "oc"):
                 table[parts[0]](*args, eng=parts[-1])
             else:

@@ -112,7 +112,7 @@ def tile_cauchytransferfunctionfilter_d2p_kernel(
         g_bf = [sb("g_bf%d" % c, [P, 512, 4], BF16) for c in range(2)]
         g_c = [sb("g_c%d" % c, [P, 512], U32) for c in range(2)]
         g_cs = [sb("g_cs%d" % c, [P, 512], U8) for c in range(2)]
-        k = sb("k", [P, 4, 2, 128, 4], F32)
+        k = sb("k", [P, 4, 2, 32, 4, 4], F32)
         p_w = sb("p_w", [P, 2, 1024], U8)
         p_s = sb("p_s", [P, 2, 512], U8)
         x_il = [sb("x_il%d" % a, [P, D, 4], U8) for a in range(4)]
@@ -158,9 +158,9 @@ def tile_cauchytransferfunctionfilter_d2p_kernel(
 
         def gi(t):
             nc.vector.tensor_tensor(
-                out=g_bf[1][:, cols(t), :],
-                in0=banks["de", t][:].rearrange("p (t m) -> p m t", t=4),
-                in1=w[:, :, cols(t)].rearrange("p t m -> p m t"),
+                out=g_bf[1][:, cols(t), :].rearrange("p (g i) t -> p g t i", i=4),
+                in0=quads(banks["de", t][:]),
+                in1=w[:, :, cols(t)].rearrange("p t (g i) -> p g t i", i=4),
                 op=ALU.mult,
             )
 
@@ -183,7 +183,7 @@ def tile_cauchytransferfunctionfilter_d2p_kernel(
                 )
 
         def kc(blk, c):
-            nc.scalar.copy(out=k[:, blk, c, :, :], in_=banks["k", blk, c][:].rearrange("p (t d) -> p d t", t=4))
+            nc.scalar.copy(out=k[:, blk, c], in_=quads(banks["k", blk, c][:]))
 
         def pw(g):
             nc.vector.tensor_copy(
@@ -251,15 +251,19 @@ def tile_cauchytransferfunctionfilter_d2p_kernel(
                     )
 
 
+        def quads(ap):
+            return ap.rearrange("p (t g i) -> p g t i", t=4, i=4)
+
         def tt(i, blk):
             h = blk // 2
-            dst = f_bf[i][h][:, blk % 2] if (i, h) == (1, 1) else f_bf[i][h][:, :, blk % 2]
-            nc.vector.tensor_tensor(
-                out=dst,
-                in0=banks["u", i, blk][:].rearrange("p (t d) -> p d t", t=4).unsqueeze(1).to_broadcast([P, 2, 128, 4]),
-                in1=k[:, blk],
-                op=ALU.mult,
-            )
+            for c in range(2):
+                dst = f_bf[i][h][:, blk % 2, c] if (i, h) == (1, 1) else f_bf[i][h][:, c, blk % 2]
+                nc.vector.tensor_tensor(
+                    out=dst.rearrange("p (g i) t -> p g t i", i=4),
+                    in0=quads(banks["u", i, blk][:]),
+                    in1=k[:, blk, c],
+                    op=ALU.mult,
+                )
 
         def fq(i, h, blk=None):
             if blk is None:

@@ -11,27 +11,19 @@ U8 = mybir.dt.uint8
 FP8 = mybir.dt.float8_e4m3fn
 E4M3 = mybir.dt.float8_e4m3fn_x4
 E2M1 = mybir.dt.float4_e2m1fn_x4
-ALU = mybir.AluOpType
+MULT = mybir.AluOpType.mult
 ACT = mybir.ActivationFunctionType
 
 B, S, D, M, N = 2, 1024, 512, 512, 512
 P = 128
+T = 4
+RUN = 4
+BLOCKS = D // P
+ROW_TILES = S // P
+
 FLOPS = 2 * (2 * M * N * D + B * M * S * D + 2 * B * S * M * D)
 
-ORDER = """
-de.1 de.3 xi.0 sq.1 de.2 sq.3 de.0 xi.2 sq.2 xw.0.3.S pw.1 sq.0
-ars.1 xi.3 ars.0 ars.2 tr.0 xi.1 ars.3 xw.2.1.S tr.1 w.2 xw.3.2.S xw.3.1.V
-xw.2.3.S w.1 xw.0.1.S w.0 xw.2.2.S w.3 qc.1.0 pw.0 qc.1.1 gi.1 xw.1.1.S tr.3
-ps xw.1.2.S gr xw.0.2.S xw.1.0.S gi.2 xw.1.3.S xw.2.0.S gi.0 tr.2 xw.3.0.S gi.3
-xw.0.0.S gq.0 xw.3.3.S gq.1 k.3.0 qc.3.0 xq.0 qc.3.1 k.3.1 xq.1 k.2.1 qc.0.0
-qq.1 k.2.0 kc.2.1 u.0.2 xq.3 qc.0.1 xq.2 u.0.3 kc.3.0 qq.0 kc.3.1 k.0.1
-k.1.0 qq.3 kc.2.0 u.1.1 qc.2.1 tt.0.3 k.0.0 kc.1.0 u.1.3 tt.0.2 kc.0.0 u.0.0
-kc.0.1 tt.1.3 qc.2.0 u.1.2 k.1.1 fq.0.1 u.0.1 kc.1.1 fq.1.1.3 qq.2 sy.0.1.0 sy.1.1.3.0
-tt.0.1 oc.0.1.0.S sy.0.1.1 oc.1.1.3.0.S tt.0.0 sy.0.1.3 sy.1.1.3.1 oc.0.1.3.S tt.1.2 sy.0.1.2 oc.1.1.3.1.S u.1.0
-fq.0.0 oc.0.1.2.S fq.1.1.2 oc.0.1.1.S tt.1.0 sy.0.0.2 sy.0.0.3 oc.0.0.2.S tt.1.1 sy.1.1.2.0 oc.0.0.3.S sy.1.1.2.1
-oc.1.1.2.0.S sy.0.0.1 fq.1.0 oc.1.1.2.1.S sy.0.0.0 oc.0.0.1.V sy.1.0.3 oc.0.0.0.S sy.1.0.1 oc.1.0.3.V sy.1.0.2 oc.1.0.1.V
-sy.1.0.0 oc.1.0.2.V oc.1.0.0.S
-"""
+PIECES = ((0, 0, 2), (0, 2, 2), (1, 0, 2), (1, 2, 1), (1, 3, 1))
 
 
 def tile_cauchytransferfunctionfilter_d2p_kernel(
@@ -49,291 +41,391 @@ def tile_cauchytransferfunctionfilter_d2p_kernel(
         def sb(name, shape, dt):
             return keep.tile(shape, dt, name=name, align_bytes=64)
 
-        right = sb("right", [P, 512], BF16)
-        left = sb("left", [P, 512], BF16)
-        warm = sb("warm", [P, 8], F32)
-        warm2 = sb("warm2", [P, 8], F32)
-        c_s = sb("c_s", [P, 512], U8)
-        p_s_raw = sb("p_s_raw", [P, 2, 512], U8)
-        ident = sb("ident", [P, P], F32)
-        x_raw = [sb("x_raw%d" % a, [P, 4, D], U8) for a in range(4)]
-        x_all = sb("x_all", [P, 64], F32)
-        x_s = sb("x_s", [P, 16], F32)
-        b_col = sb("b_col", [P, 4], BF16)
-        c_w = sb("c_w", [P, 1024], U8)
-        p_w_raw = sb("p_w_raw", [P, 2, 1024], U8)
-        q_raw = sb("q_raw", [P, 2, 8, M], BF16)
-        x_view = x_bytes.rearrange("i (g p t) d -> (i g) p t d", p=P, t=4)
+        def cols(n, width=P):
+            return slice(width * n, width * n + width)
 
+        def by_runs(ap):
+            return ap.rearrange("p (t g i) -> p g t i", t=T, i=RUN)
+
+        def runs_of_words(ap):
+            return ap.rearrange("p (g i) t -> p g t i", i=RUN)
+
+        left = sb("left", [P, N], BF16)
+        right = sb("right", [P, M], BF16)
+        b_col = sb("b_col", [P, T], BF16)
+        squares = sb("squares", [P, T, M], F32)
+        roots = sb("roots", [P, T, M], F32)
+        w = sb("w", [P, T, M], F32)
+        g_bf = [sb("g_bf%d" % c, [P, M, T], BF16) for c in range(2)]
+        g_codes = [sb("g_codes%d" % c, [P, M], U32) for c in range(2)]
+        g_scales = [sb("g_scales%d" % c, [P, M], U8) for c in range(2)]
+
+        c_codes = sb("c_codes", [P, 2 * D], U8)
+        c_planes = sb("c_planes", [P, D], U8)
+        transfer_kept = sb("transfer_kept", [P, BLOCKS, 2, P // RUN, T, RUN], F32)
+
+        p_raw = sb("p_raw", [P, 2, 2 * M], U8)
+        p_raw_planes = sb("p_raw_planes", [P, 2, M], U8)
+        p_codes = sb("p_codes", [P, 2, 2 * M], U8)
+        p_planes = sb("p_planes", [P, 2, M], U8)
+
+        x_raw = [[sb("x_raw%d%d" % (i, g), [P, T, D], U8) for g in range(2)] for i in range(B)]
+        x_inter = [[sb("x_inter%d%d" % (i, g), [P, D, T], U8) for g in range(2)] for i in range(B)]
+        x_bf = [sb("x_bf%d" % i, [P, 2, D * T], BF16) for i in range(B)]
+        x_codes = [sb("x_codes%d" % i, [P, 2, D], U32) for i in range(B)]
+        x_planes = [sb("x_planes%d" % i, [P, 2, D], U8) for i in range(B)]
+        xs_rows = sb("xs_rows", [P, 32], F32)
+        xs_columns = sb("xs_columns", [P, 32], F32)
+        xs_spread = sb("xs_spread", [P, 32], F32)
+        x_s = sb("x_s", [P, 32], F32)
+
+        identity = sb("identity", [P, P], F32)
+        q_raw = sb("q_raw", [P, 2, ROW_TILES, M], BF16)
+        q_bf = [sb("q_bf%d" % h, [P, 2, 4, P, T], BF16) for h in range(2)]
+        q_codes = [sb("q_codes%d" % h, [P, 2, 4 * P], U32) for h in range(2)]
+        q_planes = [sb("q_planes%d" % h, [P, 2, 4 * P], U8) for h in range(2)]
+
+        f_bf = [sb("f_bf%d" % z, [P, 2, P * PIECES[z][2], T], BF16) for z in range(len(PIECES))]
+        f_codes = [sb("f_codes%d" % z, [P, 2, P * PIECES[z][2]], U32) for z in range(len(PIECES))]
+        f_planes = [sb("f_planes%d" % z, [P, 2, P * PIECES[z][2]], U8) for z in range(len(PIECES))]
+        o_sb = [sb("o_sb%d" % z, [P, ROW_TILES, P * PIECES[z][2]], F32) for z in range(len(PIECES))]
+
+        difference_bank, transfer_bank, q_bank, u_bank = {}, {}, {}, {}
+
+        nc.gpsimd.memset(xs_rows[:], 0.0)
         nc.vector.memset(right[:], 0.0)
         nc.gpsimd.memset(left[:], 1.0)
         nc.vector.memset(right[32:33, :], -1.0)
-        nc.vector.memset(warm[:], 1.0)
-        nc.vector.memset(c_s[:].bitcast(I32), 0)
-        nc.gpsimd.memset(p_s_raw[:].rearrange("p g n -> p (g n)").bitcast(I32), 0)
+        warm_in = sb("warm_in", [P, 1], F32)
+        warm_out = sb("warm_out", [P, 1], F32)
+        nc.vector.memset(warm_in[:], 1.0)
+        nc.vector.memset(c_planes[:].bitcast(I32), 0)
+        nc.gpsimd.memset(p_raw_planes[:].rearrange("p g n -> p (g n)").bitcast(I32), 0)
 
-        nc.sync.dma_start(out=x_raw[0][:], in_=x_view[0])
+        def load_x(i, g):
+            nc.sync.dma_start(
+                out=x_raw[i][g][:], in_=x_bytes[i].rearrange("(g p t) d -> g p t d", p=P, t=T)[g]
+            )
+
+        def load_q(h, c):
+            nc.sync.dma_start(
+                out=q_raw[:, c, cols(h, 4), :],
+                in_=q[c].rearrange("(p j) m -> p j m", j=ROW_TILES)[:, cols(h, 4), :],
+            )
+
+        load_x(0, 0)
         nc.sync.dma_start(out=right[0:1, :], in_=om.rearrange("(o m) -> o m", o=1))
         nc.sync.dma_start(out=left[32:33, :], in_=nu.rearrange("(o n) -> o n", o=1))
-        nc.scalar.dma_start(out=x_all[:], in_=x_scale.rearrange("i s j -> (i s j)").partition_broadcast(P))
-        nc.scalar.dma_start(out=b_col[:], in_=b.rearrange("(p t) -> p t", t=4))
-        nc.scalar.activation(out=warm2[:], in_=warm[:], func=ACT.Abs_reciprocal_sqrt, bias=0.25)
-        for quad in range(4):
-            nc.scalar.dma_start(
-                out=c_s[32 * quad : 32 * quad + 4, :].bitcast(I32),
-                in_=c_scales[0, 4 * quad : 4 * quad + 4, :].bitcast(I32),
-            )
-        for a in range(1, 4):
-            nc.sync.dma_start(out=x_raw[a][:], in_=x_view[a])
-        nc.sync.dma_start(out=p_w_raw[:].bitcast(I32), in_=p_words.rearrange("g p n -> p g n").bitcast(I32))
+        nc.scalar.dma_start(
+            out=xs_rows[0:128:32, 0:16].rearrange("a (n j) -> a n j", j=BLOCKS),
+            in_=x_scale.rearrange("i (g a) j -> a (i g) j", a=4),
+        )
+        nc.scalar.dma_start(out=b_col[:], in_=b.rearrange("(p t) -> p t", t=T))
+        nc.scalar.activation(out=warm_out[:], in_=warm_in[:], func=ACT.Abs_reciprocal_sqrt)
+        load_x(0, 1)
+        load_x(1, 0)
+        load_x(1, 1)
+        nc.sync.dma_start(out=p_raw[:].bitcast(I32), in_=p_words.rearrange("g p n -> p g n").bitcast(I32))
+        load_q(0, 0)
+        load_q(0, 1)
+        load_q(1, 0)
+        nc.sync.dma_start(out=c_codes[:].bitcast(I32), in_=c_words[0].bitcast(I32))
         for quad in range(4):
             nc.sync.dma_start(
-                out=p_s_raw[32 * quad : 32 * quad + 4, :, :].bitcast(I32),
-                in_=p_scales[:, 4 * quad : 4 * quad + 4, :].rearrange("g r n -> r g n").bitcast(I32),
+                out=p_raw_planes[32 * quad : 32 * quad + 4, :, :].bitcast(I32),
+                in_=p_scales[:, cols(quad, 4), :].rearrange("g r n -> r g n").bitcast(I32),
             )
-        nc.sync.dma_start(out=c_w[:].bitcast(I32), in_=c_words[0].bitcast(I32))
-        for h in range(2):
-            for c in range(2):
-                nc.sync.dma_start(
-                    out=q_raw[:, c, 4 * h : 4 * h + 4, :],
-                    in_=q[c].rearrange("(p j) m -> p j m", j=8)[:, 4 * h : 4 * h + 4, :],
-                )
         for quad in range(4):
-            rows = slice(32 * quad, 32 * quad + 32)
-            nc.gpsimd.tensor_copy(
-                out=x_s[rows, :].rearrange("p (a j) -> p a j", j=4),
-                in_=x_all[rows, :].rearrange("p (a s j) -> p a s j", s=4, j=4)[:, :, quad, :],
+            nc.sync.dma_start(
+                out=c_planes[32 * quad : 32 * quad + 4, :].bitcast(I32),
+                in_=c_scales[0, cols(quad, 4), :].bitcast(I32),
             )
-        make_identity(nc, ident[:])
+        load_q(1, 1)
+        make_identity(nc, identity[:])
 
-        sq = sb("sq", [P, 4, 512], F32)
-        root = sb("root", [P, 4, 512], F32)
-        w = sb("w", [P, 4, 512], F32)
-        g_bf = [sb("g_bf%d" % c, [P, 512, 4], BF16) for c in range(2)]
-        g_c = [sb("g_c%d" % c, [P, 512], U32) for c in range(2)]
-        g_cs = [sb("g_cs%d" % c, [P, 512], U8) for c in range(2)]
-        k = sb("k", [P, 4, 2, 32, 4, 4], F32)
-        p_w = sb("p_w", [P, 2, 1024], U8)
-        p_s = sb("p_s", [P, 2, 512], U8)
-        x_il = [sb("x_il%d" % a, [P, D, 4], U8) for a in range(4)]
-        x_bf = [sb("x_bf%d" % a, [P, D * 4], BF16) for a in range(4)]
-        x_c = [sb("x_c%d" % i, [P, 2, D], U32) for i in range(2)]
-        x_cs = [sb("x_cs%d" % i, [P, 2, D], U8) for i in range(2)]
-        q_bf = [sb("q_bf%d" % n, [P, 4, 128, 4], BF16) for n in range(4)]
-        q_c = [sb("q_c%d" % n, [P, 512], U32) for n in range(4)]
-        q_cs = [sb("q_cs%d" % n, [P, 512], U8) for n in range(4)]
-        q_words = q_raw[:].rearrange("p c j m -> p (c j m)").bitcast(F32)
-        f_bf = [[sb("f_bf%d%d" % (i, h), [P, 2, 2, 128, 4], BF16) for h in range(2)] for i in range(2)]
-        f_c = [[sb("f_c%d%d" % (i, h), [P, 2, 2, 128], U32) for h in range(2)] for i in range(2)]
-        f_cs = [[sb("f_cs%d%d" % (i, h), [P, 2, 2, 128], U8) for h in range(2)] for i in range(2)]
-        o = [[sb("o%d%d" % (i, h), [P, 8, 256], F32) for h in range(2)] for i in range(2)]
-        banks = {}
+        def difference(tm):
+            d = difference_bank[tm] = bank("difference%d" % tm)
+            for t in range(T):
+                nc.tensor.matmul(d[:, cols(t)], lhsT=left[:, t::T], rhs=right[:, tm::T], start=True, stop=True)
 
-        def cols(n, width=128):
-            return slice(width * n, width * n + width)
-
-        def de(t):
-            d = banks["de", t] = bank("de%d" % t)
-            for tn in range(4):
-                nc.tensor.matmul(d[:, cols(tn)], lhsT=left[:, tn::4], rhs=right[:, t::4], start=True, stop=True)
-
-        def do_sq(t):
+        def square(tm):
             nc.scalar.activation(
-                out=sq[:, :, cols(t)], in_=banks["de", t][:].rearrange("p (t m) -> p t m", t=4), func=ACT.Square
+                out=squares[:, :, cols(tm)],
+                in_=difference_bank[tm][:].rearrange("p (t m) -> p t m", t=T),
+                func=ACT.Square,
             )
 
-        def ars(t):
-            nc.scalar.activation(out=root[:, :, cols(t)], in_=sq[:, :, cols(t)], func=ACT.Abs_reciprocal_sqrt, bias=0.25)
+        def inverse_root(half):
+            ms = cols(half, 2 * P)
+            nc.scalar.activation(
+                out=roots[:, :, ms], in_=squares[:, :, ms], func=ACT.Abs_reciprocal_sqrt, bias=0.25
+            )
 
-        def do_w(t):
+        def weight(t):
             nc.vector.scalar_tensor_tensor(
-                out=w[:, t, :], in0=root[:, t, :], scalar=b_col[:, t : t + 1], in1=root[:, t, :],
-                op0=ALU.mult, op1=ALU.mult,
+                out=w[:, t, :], in0=roots[:, t, :], scalar=b_col[:, t : t + 1], in1=roots[:, t, :], op0=MULT, op1=MULT
             )
 
-        def gr():
-            nc.vector.tensor_scalar(
-                out=g_bf[0][:], in0=w[:].rearrange("p t m -> p m t"), scalar1=0.5, scalar2=None, op0=ALU.mult
-            )
-
-        def gi(t):
+        def g_imaginary(tm):
             nc.vector.tensor_tensor(
-                out=g_bf[1][:, cols(t), :].rearrange("p (g i) t -> p g t i", i=4),
-                in0=quads(banks["de", t][:]),
-                in1=w[:, :, cols(t)].rearrange("p t (g i) -> p g t i", i=4),
-                op=ALU.mult,
+                out=runs_of_words(g_bf[1][:, cols(tm), :]),
+                in0=by_runs(difference_bank[tm][:]),
+                in1=w[:, :, cols(tm)].rearrange("p t (g i) -> p g t i", i=RUN),
+                op=MULT,
             )
 
-        def gq(c):
+        def g_real():
+            nc.vector.tensor_scalar(
+                out=runs_of_words(g_bf[0][:]),
+                in0=w[:].rearrange("p t (g i) -> p g t i", i=RUN),
+                scalar1=0.5,
+                scalar2=None,
+                op0=MULT,
+            )
+
+        def g_quantize(c):
             nc.vector.quantize_mx(
-                out=g_c[c][:].bitcast(E4M3), scales=g_cs[c][:], in_=g_bf[c][:].rearrange("p m t -> p (m t)")
+                out=g_codes[c][:].bitcast(E4M3), scales=g_scales[c][:], in_=g_bf[c][:].rearrange("p m t -> p (m t)")
             )
 
-        def do_k(blk, c):
-            kb = banks["k", blk, c] = bank("k%d%d" % (blk, c))
-            for t in range(4):
+        def transfer(blk, c):
+            k_ps = transfer_bank[blk, c] = bank("transfer%d%d" % (blk, c))
+            for t in range(T):
                 nc.tensor.matmul_mx(
-                    out=kb[:, cols(t)],
-                    lhsT=g_c[c][:, cols(t)].bitcast(E4M3),
-                    lhsT_scale=g_cs[c][:, cols(t)],
-                    rhs=c_w[:, cols(blk, 256)].bitcast(E2M1),
-                    rhs_scale=c_s[:, cols(blk)],
+                    out=k_ps[:, cols(t)],
+                    lhsT=g_codes[c][:, cols(t)].bitcast(E4M3),
+                    lhsT_scale=g_scales[c][:, cols(t)],
+                    rhs=c_codes[:, cols(blk, 2 * P)].bitcast(E2M1),
+                    rhs_scale=c_planes[:, cols(blk)],
                     start=True,
                     stop=True,
                 )
 
-        def kc(blk, c):
-            nc.scalar.copy(out=k[:, blk, c], in_=quads(banks["k", blk, c][:]))
+        def keep_transfer(blk, c):
+            nc.scalar.copy(out=transfer_kept[:, blk, c], in_=by_runs(transfer_bank[blk, c][:]))
 
-        def pw(g):
+        def permute_p_codes(g):
             nc.vector.tensor_copy(
-                out=p_w[:, g, :].rearrange("p (t n e) -> p t n e", t=4, e=2),
-                in_=p_w_raw[:, g, :].rearrange("p (n t e) -> p t n e", t=4, e=2),
+                out=p_codes[:, g, :].rearrange("p (t n e) -> p t n e", t=T, e=2),
+                in_=p_raw[:, g, :].rearrange("p (n t e) -> p t n e", t=T, e=2),
             )
 
-        def ps():
+        def permute_p_planes():
             nc.vector.tensor_copy(
-                out=p_s[:].rearrange("p g (t n) -> p g t n", t=4),
-                in_=p_s_raw[:].rearrange("p g (n t) -> p g t n", t=4),
+                out=p_planes[:].rearrange("p g (t n) -> p g t n", t=T),
+                in_=p_raw_planes[:].rearrange("p g (n t) -> p g t n", t=T),
             )
 
-        def xi(a):
-            nc.vector.tensor_copy(out=x_il[a][:], in_=x_raw[a][:].rearrange("p t d -> p d t"))
+        def scales_to_columns():
+            nc.vector.transpose(out=xs_columns[:], in_=xs_rows[:])
 
-        def xw(a, j, eng="S"):
-            src = x_il[a][:].rearrange("p d t -> p (d t)")[:, cols(j, 512)].bitcast(FP8)
-            dst = x_bf[a][:, cols(j, 512)]
-            scale = x_s[:, 4 * a + j : 4 * a + j + 1]
-            if eng == "V":
-                nc.vector.tensor_scalar(out=dst, in0=src, scalar1=scale, scalar2=None, op0=ALU.mult)
-            else:
-                nc.scalar.activation(out=dst, in_=src, func=ACT.Copy, scale=scale)
+        def scales_repeat():
+            nc.vector.tensor_copy(out=xs_spread[:], in_=xs_columns[:, 0:1].to_broadcast([P, 32]))
 
-        def xq(a):
-            i, g = a // 2, a % 2
-            nc.vector.quantize_mx(out=x_c[i][:, g, :].bitcast(E4M3), scales=x_cs[i][:, g, :], in_=x_bf[a][:])
+        def scales_to_rows():
+            nc.vector.transpose(out=x_s[:], in_=xs_spread[:])
 
-        def tr(n):
-            h, c = n // 2, n % 2
-            for pair in range(2):
-                tb = banks["tr", n, pair] = bank("tr%d%d" % (n, pair))
-                for s in range(2):
-                    base = (c * 8 + 4 * h + 2 * pair + s) * 256
-                    for u in range(2):
-                        nc.tensor.transpose(tb[:, cols(2 * s + u)], q_words[:, base + u : base + 256 : 2], ident[:])
-
-        def qc(n, pair):
-            nc.scalar.copy(
-                out=q_bf[n][:, 2 * pair : 2 * pair + 2, :, :]
-                .rearrange("p s r e -> p (s r e)")
-                .bitcast(F32)
-                .rearrange("p (s r u) -> p s r u", s=2, u=2),
-                in_=banks["tr", n, pair][:].rearrange("p (s u r) -> p s r u", s=2, u=2),
+        def x_interleave(i, g):
+            nc.vector.tensor_copy(
+                out=runs_of_words(x_inter[i][g][:]), in_=x_raw[i][g][:].rearrange("p t (g i) -> p g t i", i=RUN)
             )
 
-        def qq(n):
+        def x_widen(i, g):
+            codes = x_inter[i][g][:].rearrange("p d t -> p (d t)")
+            for blk in range(BLOCKS):
+                ds = cols(blk, P * T)
+                column = BLOCKS * (2 * i + g) + blk
+                nc.scalar.activation(
+                    out=x_bf[i][:, g, ds],
+                    in_=codes[:, ds].bitcast(FP8),
+                    func=ACT.Copy,
+                    scale=x_s[:, column : column + 1],
+                )
+
+        def x_quantize(i):
             nc.vector.quantize_mx(
-                out=q_c[n][:].bitcast(E4M3), scales=q_cs[n][:], in_=q_bf[n][:].rearrange("p s r e -> p (s r e)")
+                out=x_codes[i][:].rearrange("p g d -> p (g d)").bitcast(E4M3),
+                scales=x_planes[i][:].rearrange("p g d -> p (g d)"),
+                in_=x_bf[i][:].rearrange("p g e -> p (g e)"),
             )
 
-        def do_u(i, blk):
-            ub = banks["u", i, blk] = bank("u%d%d" % (i, blk))
-            for t in range(4):
+        def analysis(i, blk):
+            u_ps = u_bank[i, blk] = bank("u%d%d" % (i, blk))
+            for t in range(T):
                 for g in range(2):
                     nc.tensor.matmul_mx(
-                        out=ub[:, cols(t)],
-                        lhsT=p_w[:, g, cols(t, 256)].bitcast(E2M1),
-                        lhsT_scale=p_s[:, g, cols(t)],
-                        rhs=x_c[i][:, g, cols(blk)].bitcast(E4M3),
-                        rhs_scale=x_cs[i][:, g, cols(blk)],
+                        out=u_ps[:, cols(t)],
+                        lhsT=p_codes[:, g, cols(t, 2 * P)].bitcast(E2M1),
+                        lhsT_scale=p_planes[:, g, cols(t)],
+                        rhs=x_codes[i][:, g, cols(blk)].bitcast(E4M3),
+                        rhs_scale=x_planes[i][:, g, cols(blk)],
                         start=(g == 0),
                         stop=(g == 1),
                     )
 
+        q_pairs = q_raw[:].rearrange("p c j m -> p (c j m)").bitcast(F32)
 
-        def quads(ap):
-            return ap.rearrange("p (t g i) -> p g t i", t=4, i=4)
+        def q_turn(h, c):
+            for pair in range(2):
+                turned = q_bank[h, c, pair] = bank("turned%d%d%d" % (h, c, pair))
+                for s in range(2):
+                    first = (ROW_TILES * c + 4 * h + 2 * pair + s) * (M // 2)
+                    for u in range(2):
+                        nc.tensor.transpose(
+                            turned[:, cols(2 * s + u)], q_pairs[:, first + u : first + M // 2 : 2], identity[:]
+                        )
 
-        def tt(i, blk):
-            h = blk // 2
+        def q_copy(h, c):
+            for pair in range(2):
+                nc.scalar.copy(
+                    out=q_bf[h][:, c, cols(pair, 2)]
+                    .rearrange("p s r e -> p (s r e)")
+                    .bitcast(F32)
+                    .rearrange("p (s r u) -> p s r u", s=2, u=2),
+                    in_=q_bank[h, c, pair][:].rearrange("p (s u r) -> p s r u", s=2, u=2),
+                )
+
+        def q_quantize(h):
+            nc.vector.quantize_mx(
+                out=q_codes[h][:].rearrange("p c r -> p (c r)").bitcast(E4M3),
+                scales=q_planes[h][:].rearrange("p c r -> p (c r)"),
+                in_=q_bf[h][:].rearrange("p c s r e -> p (c s r e)"),
+            )
+
+        def filter_part(z, blk, c):
+            i, first = PIECES[z][:2]
+            nc.vector.tensor_tensor(
+                out=runs_of_words(f_bf[z][:, c, cols(blk - first), :]),
+                in0=by_runs(u_bank[i, blk][:]),
+                in1=transfer_kept[:, blk, c],
+                op=MULT,
+            )
+
+        def filter_block(z, blk):
             for c in range(2):
-                dst = f_bf[i][h][:, blk % 2, c] if (i, h) == (1, 1) else f_bf[i][h][:, c, blk % 2]
-                nc.vector.tensor_tensor(
-                    out=dst.rearrange("p (g i) t -> p g t i", i=4),
-                    in0=quads(banks["u", i, blk][:]),
-                    in1=k[:, blk, c],
-                    op=ALU.mult,
-                )
+                filter_part(z, blk, c)
 
-        def fq(i, h, blk=None):
-            if blk is None:
-                nc.vector.quantize_mx(
-                    out=f_c[i][h][:].rearrange("p a b d -> p (a b d)").bitcast(E4M3),
-                    scales=f_cs[i][h][:].rearrange("p a b d -> p (a b d)"),
-                    in_=f_bf[i][h][:].rearrange("p a b d t -> p (a b d t)"),
-                )
-            else:
-                nc.vector.quantize_mx(
-                    out=f_c[i][h][:, blk % 2].rearrange("p c d -> p (c d)").bitcast(E4M3),
-                    scales=f_cs[i][h][:, blk % 2].rearrange("p c d -> p (c d)"),
-                    in_=f_bf[i][h][:, blk % 2].rearrange("p c d t -> p (c d t)"),
-                )
+        def f_quantize(z):
+            nc.vector.quantize_mx(
+                out=f_codes[z][:].rearrange("p c d -> p (c d)").bitcast(E4M3),
+                scales=f_planes[z][:].rearrange("p c d -> p (c d)"),
+                in_=f_bf[z][:].rearrange("p c d t -> p (c d t)"),
+            )
 
-        def q_at(j, c):
-            n = 2 * (j // 4) + c
-            return q_c[n][:, cols(j % 4)].bitcast(E4M3), q_cs[n][:, cols(j % 4)]
-
-        def sy(i, h, m, part=None):
-            if part is None:
-                ob = banks["sy", i, h, m] = bank("sy%d%d%d" % (i, h, m))
-                tiles, width = (2 * m, 2 * m + 1), 256
-            else:
-                blk, m = m, part
-                ob = banks["sy", i, h, blk, m] = bank("sy%d%d%d%d" % (i, h, blk, m))
-                tiles, width = (4 * m, 4 * m + 1, 4 * m + 2, 4 * m + 3), 128
-            for s in range(len(tiles)):
+        def synthesis(z, m, copy=nc.scalar.copy):
+            i, first, blocks = PIECES[z]
+            width = P * blocks
+            tiles = 512 // width
+            o_ps = bank("o%d%d" % (z, m))
+            for s in range(tiles):
+                j = tiles * m + s
                 for c in range(2):
-                    codes, scales = q_at(tiles[s], c)
-                    if part is None:
-                        fc = f_c[i][h][:, c].rearrange("p b d -> p (b d)")
-                        fs = f_cs[i][h][:, c].rearrange("p b d -> p (b d)")
-                    else:
-                        fc = f_c[i][h][:, blk % 2, c]
-                        fs = f_cs[i][h][:, blk % 2, c]
                     nc.tensor.matmul_mx(
-                        out=ob[:, cols(s, width)],
-                        lhsT=codes,
-                        lhsT_scale=scales,
-                        rhs=fc.bitcast(E4M3),
-                        rhs_scale=fs,
+                        out=o_ps[:, cols(s, width)],
+                        lhsT=q_codes[j // 4][:, c, cols(j % 4)].bitcast(E4M3),
+                        lhsT_scale=q_planes[j // 4][:, c, cols(j % 4)],
+                        rhs=f_codes[z][:, c, :].bitcast(E4M3),
+                        rhs_scale=f_planes[z][:, c, :],
                         start=(c == 0),
                         stop=(c == 1),
                     )
+            copy(out=o_sb[z][:, cols(m, tiles), :], in_=o_ps[:].rearrange("p (j d) -> p j d", d=width))
+            nc.sync.dma_start(
+                out=out[i].rearrange("(p j) d -> p j d", j=ROW_TILES)[
+                    :, cols(m, tiles), P * first : P * first + width
+                ],
+                in_=o_sb[z][:, cols(m, tiles), :],
+            )
 
-        def oc(i, h, m, part=None, eng="S"):
-            if part is None:
-                src = banks["sy", i, h, m][:].rearrange("p (j d) -> p j d", j=2)
-                js, ds, do = slice(2 * m, 2 * m + 2), slice(256 * h, 256 * h + 256), slice(0, 256)
-            else:
-                blk, m = m, part
-                src = banks["sy", i, h, blk, m][:].rearrange("p (j d) -> p j d", j=4)
-                js, ds, do = slice(4 * m, 4 * m + 4), cols(blk), cols(blk % 2)
-            dst = o[i][h][:, js, do]
-            if eng == "V":
-                nc.vector.tensor_copy(out=dst, in_=src)
-            else:
-                nc.scalar.copy(out=dst, in_=src)
-            nc.sync.dma_start(out=out[i].rearrange("(p j) d -> p j d", j=8)[:, js, ds], in_=dst)
+        for tm in range(T):
+            difference(tm)
+        for tm in range(T):
+            square(tm)
+        for half in range(2):
+            inverse_root(half)
 
-        table = {
-            "de": de, "sq": do_sq, "ars": ars, "w": do_w, "gr": gr, "gi": gi, "gq": gq, "k": do_k, "kc": kc,
-            "pw": pw, "ps": ps, "xi": xi, "xw": xw, "xq": xq, "tr": tr, "qc": qc, "qq": qq, "u": do_u,
-            "tt": tt, "fq": fq, "sy": sy, "oc": oc,
-        }
-        for step in ORDER.split():
-            parts = step.split(".")
-            args = [int(z) for z in parts[1:] if z not in ("S", "V", "G")]
-            if parts[0] in ("xw", "oc"):
-                table[parts[0]](*args, eng=parts[-1])
-            else:
-                table[parts[0]](*args)
+        x_interleave(0, 0)
+        scales_to_columns()
+        x_interleave(0, 1)
+        scales_repeat()
+        x_interleave(1, 0)
+        scales_to_rows()
+        x_interleave(1, 1)
+        permute_p_codes(0)
+        for t in range(T):
+            weight(t)
+        permute_p_codes(1)
+        for tm in range(T):
+            g_imaginary(tm)
+        g_real()
+
+        x_widen(0, 0)
+        x_widen(0, 1)
+        q_turn(0, 0)
+        q_turn(0, 1)
+        q_copy(0, 0)
+        q_copy(0, 1)
+        x_widen(1, 0)
+        q_turn(1, 0)
+
+        g_quantize(1)
+        permute_p_planes()
+        g_quantize(0)
+        x_quantize(0)
+        q_quantize(0)
+
+        for c in (1, 0):
+            for blk in (0, 1):
+                transfer(blk, c)
+                keep_transfer(blk, c)
+        analysis(0, 0)
+        analysis(0, 1)
+        x_widen(1, 1)
+        for c in (1, 0):
+            transfer(2, c)
+            keep_transfer(2, c)
+        q_turn(1, 1)
+        q_copy(1, 0)
+        q_copy(1, 1)
+        analysis(0, 2)
+        for c in (1, 0):
+            transfer(3, c)
+            keep_transfer(3, c)
+        analysis(0, 3)
+
+        filter_block(0, 0)
+        filter_block(0, 1)
+        f_quantize(0)
+        x_quantize(1)
+        filter_block(1, 2)
+        q_quantize(1)
+        filter_block(1, 3)
+
+        analysis(1, 0)
+        synthesis(0, 0)
+        synthesis(0, 1)
+        analysis(1, 1)
+        filter_part(2, 0, 0)
+        f_quantize(1)
+        filter_part(2, 0, 1)
+        filter_block(2, 1)
+        synthesis(0, 2)
+        synthesis(0, 3)
+        analysis(1, 2)
+        synthesis(1, 0)
+        synthesis(1, 1)
+        analysis(1, 3)
+        filter_part(3, 2, 0)
+        f_quantize(2)
+        filter_part(3, 2, 1)
+        filter_part(4, 3, 0)
+        f_quantize(3)
+        filter_part(4, 3, 1)
+        f_quantize(4)
+        synthesis(1, 2)
+        synthesis(1, 3)
+        for m in range(4):
+            synthesis(2, m)
+        for z in (3, 4):
+            synthesis(z, 0, nc.vector.tensor_copy)
+            synthesis(z, 1)

from contextlib import ExitStack

import concourse.mybir as mybir
from concourse.masks import make_identity

F32 = mybir.dt.float32
BF16 = mybir.dt.bfloat16
U32 = mybir.dt.uint32
I32 = mybir.dt.int32
U8 = mybir.dt.uint8
FP8 = mybir.dt.float8_e4m3fn
E4M3 = mybir.dt.float8_e4m3fn_x4
E2M1 = mybir.dt.float4_e2m1fn_x4
MULT = mybir.AluOpType.mult
ACT = mybir.ActivationFunctionType

B, S, D, M, N = 2, 1024, 512, 512, 512
P = 128
T = 4
RUN = 4
BLOCKS = D // P
ROW_TILES = S // P

FLOPS = 2 * (2 * M * N * D + B * M * S * D + 2 * B * S * M * D)

PIECES = ((0, 0, 2), (0, 2, 2), (1, 0, 2), (1, 2, 1), (1, 3, 1))


def tile_cauchytransferfunctionfilter_d2p_kernel(
    tc, x_bytes, x_scale, p_words, p_scales, om, nu, b, c_words, c_scales, q, out
):
    nc = tc.nc
    with ExitStack() as ctx:
        keep = ctx.enter_context(tc.tile_pool(name="keep", bufs=1))
        psum = ctx.enter_context(tc.psum_pool(name="psum", bufs=8))
        ctx.enter_context(tc.manual_schedule())

        def bank(name):
            return psum.tile([P, 512], F32, tag="bank", name=name)

        def sb(name, shape, dt):
            return keep.tile(shape, dt, name=name, align_bytes=64)

        def cols(n, width=P):
            return slice(width * n, width * n + width)

        def by_runs(ap):
            return ap.rearrange("p (t g i) -> p g t i", t=T, i=RUN)

        def runs_of_words(ap):
            return ap.rearrange("p (g i) t -> p g t i", i=RUN)

        left = sb("left", [P, N], BF16)
        right = sb("right", [P, M], BF16)
        b_col = sb("b_col", [P, T], BF16)
        squares = sb("squares", [P, T, M], F32)
        roots = sb("roots", [P, T, M], F32)
        w = sb("w", [P, T, M], F32)
        g_bf = [sb("g_bf%d" % c, [P, M, T], BF16) for c in range(2)]
        g_codes = [sb("g_codes%d" % c, [P, M], U32) for c in range(2)]
        g_scales = [sb("g_scales%d" % c, [P, M], U8) for c in range(2)]

        c_codes = sb("c_codes", [P, 2 * D], U8)
        c_planes = sb("c_planes", [P, D], U8)
        transfer_kept = sb("transfer_kept", [P, BLOCKS, 2, P // RUN, T, RUN], F32)

        p_raw = sb("p_raw", [P, 2, 2 * M], U8)
        p_raw_planes = sb("p_raw_planes", [P, 2, M], U8)
        p_codes = sb("p_codes", [P, 2, 2 * M], U8)
        p_planes = sb("p_planes", [P, 2, M], U8)

        x_raw = [[sb("x_raw%d%d" % (i, g), [P, T, D], U8) for g in range(2)] for i in range(B)]
        x_inter = [[sb("x_inter%d%d" % (i, g), [P, D, T], U8) for g in range(2)] for i in range(B)]
        x_bf = [sb("x_bf%d" % i, [P, 2, D * T], BF16) for i in range(B)]
        x_codes = [sb("x_codes%d" % i, [P, 2, D], U32) for i in range(B)]
        x_planes = [sb("x_planes%d" % i, [P, 2, D], U8) for i in range(B)]
        xs_rows = sb("xs_rows", [P, 32], F32)
        xs_columns = sb("xs_columns", [P, 32], F32)
        xs_spread = sb("xs_spread", [P, 32], F32)
        x_s = sb("x_s", [P, 32], F32)

        identity = sb("identity", [P, P], F32)
        q_raw = sb("q_raw", [P, 2, ROW_TILES, M], BF16)
        q_bf = [sb("q_bf%d" % h, [P, 2, 4, P, T], BF16) for h in range(2)]
        q_codes = [sb("q_codes%d" % h, [P, 2, 4 * P], U32) for h in range(2)]
        q_planes = [sb("q_planes%d" % h, [P, 2, 4 * P], U8) for h in range(2)]

        f_bf = [sb("f_bf%d" % z, [P, 2, P * PIECES[z][2], T], BF16) for z in range(len(PIECES))]
        f_codes = [sb("f_codes%d" % z, [P, 2, P * PIECES[z][2]], U32) for z in range(len(PIECES))]
        f_planes = [sb("f_planes%d" % z, [P, 2, P * PIECES[z][2]], U8) for z in range(len(PIECES))]
        o_sb = [sb("o_sb%d" % z, [P, ROW_TILES, P * PIECES[z][2]], F32) for z in range(len(PIECES))]

        difference_bank, transfer_bank, q_bank, u_bank = {}, {}, {}, {}

        nc.gpsimd.memset(xs_rows[:], 0.0)
        nc.vector.memset(right[:], 0.0)
        nc.gpsimd.memset(left[:], 1.0)
        nc.vector.memset(right[32:33, :], -1.0)
        warm_in = sb("warm_in", [P, 1], F32)
        warm_out = sb("warm_out", [P, 1], F32)
        nc.vector.memset(warm_in[:], 1.0)
        nc.vector.memset(c_planes[:].bitcast(I32), 0)
        nc.gpsimd.memset(p_raw_planes[:].rearrange("p g n -> p (g n)").bitcast(I32), 0)

        def load_x(i, g):
            nc.sync.dma_start(
                out=x_raw[i][g][:], in_=x_bytes[i].rearrange("(g p t) d -> g p t d", p=P, t=T)[g]
            )

        def load_q(h, c):
            nc.sync.dma_start(
                out=q_raw[:, c, cols(h, 4), :],
                in_=q[c].rearrange("(p j) m -> p j m", j=ROW_TILES)[:, cols(h, 4), :],
            )

        load_x(0, 0)
        nc.sync.dma_start(out=right[0:1, :], in_=om.rearrange("(o m) -> o m", o=1))
        nc.sync.dma_start(out=left[32:33, :], in_=nu.rearrange("(o n) -> o n", o=1))
        nc.scalar.dma_start(
            out=xs_rows[0:128:32, 0:16].rearrange("a (n j) -> a n j", j=BLOCKS),
            in_=x_scale.rearrange("i (g a) j -> a (i g) j", a=4),
        )
        nc.scalar.dma_start(out=b_col[:], in_=b.rearrange("(p t) -> p t", t=T))
        nc.scalar.activation(out=warm_out[:], in_=warm_in[:], func=ACT.Abs_reciprocal_sqrt)
        load_x(0, 1)
        load_x(1, 0)
        load_x(1, 1)
        nc.sync.dma_start(out=p_raw[:].bitcast(I32), in_=p_words.rearrange("g p n -> p g n").bitcast(I32))
        load_q(0, 0)
        load_q(0, 1)
        load_q(1, 0)
        nc.sync.dma_start(out=c_codes[:].bitcast(I32), in_=c_words[0].bitcast(I32))
        for quad in range(4):
            nc.sync.dma_start(
                out=p_raw_planes[32 * quad : 32 * quad + 4, :, :].bitcast(I32),
                in_=p_scales[:, cols(quad, 4), :].rearrange("g r n -> r g n").bitcast(I32),
            )
        for quad in range(4):
            nc.sync.dma_start(
                out=c_planes[32 * quad : 32 * quad + 4, :].bitcast(I32),
                in_=c_scales[0, cols(quad, 4), :].bitcast(I32),
            )
        load_q(1, 1)
        make_identity(nc, identity[:])

        def difference(tm):
            d = difference_bank[tm] = bank("difference%d" % tm)
            for t in range(T):
                nc.tensor.matmul(d[:, cols(t)], lhsT=left[:, t::T], rhs=right[:, tm::T], start=True, stop=True)

        def square(tm):
            nc.scalar.activation(
                out=squares[:, :, cols(tm)],
                in_=difference_bank[tm][:].rearrange("p (t m) -> p t m", t=T),
                func=ACT.Square,
            )

        def inverse_root(half):
            ms = cols(half, 2 * P)
            nc.scalar.activation(
                out=roots[:, :, ms], in_=squares[:, :, ms], func=ACT.Abs_reciprocal_sqrt, bias=0.25
            )

        def weight(t):
            nc.vector.scalar_tensor_tensor(
                out=w[:, t, :], in0=roots[:, t, :], scalar=b_col[:, t : t + 1], in1=roots[:, t, :], op0=MULT, op1=MULT
            )

        def g_imaginary(tm):
            nc.vector.tensor_tensor(
                out=runs_of_words(g_bf[1][:, cols(tm), :]),
                in0=by_runs(difference_bank[tm][:]),
                in1=w[:, :, cols(tm)].rearrange("p t (g i) -> p g t i", i=RUN),
                op=MULT,
            )

        def g_real():
            nc.vector.tensor_scalar(
                out=runs_of_words(g_bf[0][:]),
                in0=w[:].rearrange("p t (g i) -> p g t i", i=RUN),
                scalar1=0.5,
                scalar2=None,
                op0=MULT,
            )

        def g_quantize(c):
            nc.vector.quantize_mx(
                out=g_codes[c][:].bitcast(E4M3), scales=g_scales[c][:], in_=g_bf[c][:].rearrange("p m t -> p (m t)")
            )

        def transfer(blk, c):
            k_ps = transfer_bank[blk, c] = bank("transfer%d%d" % (blk, c))
            for t in range(T):
                nc.tensor.matmul_mx(
                    out=k_ps[:, cols(t)],
                    lhsT=g_codes[c][:, cols(t)].bitcast(E4M3),
                    lhsT_scale=g_scales[c][:, cols(t)],
                    rhs=c_codes[:, cols(blk, 2 * P)].bitcast(E2M1),
                    rhs_scale=c_planes[:, cols(blk)],
                    start=True,
                    stop=True,
                )

        def keep_transfer(blk, c):
            nc.scalar.copy(out=transfer_kept[:, blk, c], in_=by_runs(transfer_bank[blk, c][:]))

        def permute_p_codes(g):
            nc.vector.tensor_copy(
                out=p_codes[:, g, :].rearrange("p (t n e) -> p t n e", t=T, e=2),
                in_=p_raw[:, g, :].rearrange("p (n t e) -> p t n e", t=T, e=2),
            )

        def permute_p_planes():
            nc.vector.tensor_copy(
                out=p_planes[:].rearrange("p g (t n) -> p g t n", t=T),
                in_=p_raw_planes[:].rearrange("p g (n t) -> p g t n", t=T),
            )

        def scales_to_columns():
            nc.vector.transpose(out=xs_columns[:], in_=xs_rows[:])

        def scales_repeat():
            nc.vector.tensor_copy(out=xs_spread[:], in_=xs_columns[:, 0:1].to_broadcast([P, 32]))

        def scales_to_rows():
            nc.vector.transpose(out=x_s[:], in_=xs_spread[:])

        def x_interleave(i, g):
            nc.vector.tensor_copy(
                out=runs_of_words(x_inter[i][g][:]), in_=x_raw[i][g][:].rearrange("p t (g i) -> p g t i", i=RUN)
            )

        def x_widen(i, g):
            codes = x_inter[i][g][:].rearrange("p d t -> p (d t)")
            for blk in range(BLOCKS):
                ds = cols(blk, P * T)
                column = BLOCKS * (2 * i + g) + blk
                nc.scalar.activation(
                    out=x_bf[i][:, g, ds],
                    in_=codes[:, ds].bitcast(FP8),
                    func=ACT.Copy,
                    scale=x_s[:, column : column + 1],
                )

        def x_quantize(i):
            nc.vector.quantize_mx(
                out=x_codes[i][:].rearrange("p g d -> p (g d)").bitcast(E4M3),
                scales=x_planes[i][:].rearrange("p g d -> p (g d)"),
                in_=x_bf[i][:].rearrange("p g e -> p (g e)"),
            )

        def analysis(i, blk):
            u_ps = u_bank[i, blk] = bank("u%d%d" % (i, blk))
            for t in range(T):
                for g in range(2):
                    nc.tensor.matmul_mx(
                        out=u_ps[:, cols(t)],
                        lhsT=p_codes[:, g, cols(t, 2 * P)].bitcast(E2M1),
                        lhsT_scale=p_planes[:, g, cols(t)],
                        rhs=x_codes[i][:, g, cols(blk)].bitcast(E4M3),
                        rhs_scale=x_planes[i][:, g, cols(blk)],
                        start=(g == 0),
                        stop=(g == 1),
                    )

        q_pairs = q_raw[:].rearrange("p c j m -> p (c j m)").bitcast(F32)

        def q_turn(h, c):
            for pair in range(2):
                turned = q_bank[h, c, pair] = bank("turned%d%d%d" % (h, c, pair))
                for s in range(2):
                    first = (ROW_TILES * c + 4 * h + 2 * pair + s) * (M // 2)
                    for u in range(2):
                        nc.tensor.transpose(
                            turned[:, cols(2 * s + u)], q_pairs[:, first + u : first + M // 2 : 2], identity[:]
                        )

        def q_copy(h, c):
            for pair in range(2):
                nc.scalar.copy(
                    out=q_bf[h][:, c, cols(pair, 2)]
                    .rearrange("p s r e -> p (s r e)")
                    .bitcast(F32)
                    .rearrange("p (s r u) -> p s r u", s=2, u=2),
                    in_=q_bank[h, c, pair][:].rearrange("p (s u r) -> p s r u", s=2, u=2),
                )

        def q_quantize(h):
            nc.vector.quantize_mx(
                out=q_codes[h][:].rearrange("p c r -> p (c r)").bitcast(E4M3),
                scales=q_planes[h][:].rearrange("p c r -> p (c r)"),
                in_=q_bf[h][:].rearrange("p c s r e -> p (c s r e)"),
            )

        def filter_part(z, blk, c):
            i, first = PIECES[z][:2]
            nc.vector.tensor_tensor(
                out=runs_of_words(f_bf[z][:, c, cols(blk - first), :]),
                in0=by_runs(u_bank[i, blk][:]),
                in1=transfer_kept[:, blk, c],
                op=MULT,
            )

        def filter_block(z, blk):
            for c in range(2):
                filter_part(z, blk, c)

        def f_quantize(z):
            nc.vector.quantize_mx(
                out=f_codes[z][:].rearrange("p c d -> p (c d)").bitcast(E4M3),
                scales=f_planes[z][:].rearrange("p c d -> p (c d)"),
                in_=f_bf[z][:].rearrange("p c d t -> p (c d t)"),
            )

        def synthesis(z, m, copy=nc.scalar.copy):
            i, first, blocks = PIECES[z]
            width = P * blocks
            tiles = 512 // width
            o_ps = bank("o%d%d" % (z, m))
            for s in range(tiles):
                j = tiles * m + s
                for c in range(2):
                    nc.tensor.matmul_mx(
                        out=o_ps[:, cols(s, width)],
                        lhsT=q_codes[j // 4][:, c, cols(j % 4)].bitcast(E4M3),
                        lhsT_scale=q_planes[j // 4][:, c, cols(j % 4)],
                        rhs=f_codes[z][:, c, :].bitcast(E4M3),
                        rhs_scale=f_planes[z][:, c, :],
                        start=(c == 0),
                        stop=(c == 1),
                    )
            copy(out=o_sb[z][:, cols(m, tiles), :], in_=o_ps[:].rearrange("p (j d) -> p j d", d=width))
            nc.sync.dma_start(
                out=out[i].rearrange("(p j) d -> p j d", j=ROW_TILES)[
                    :, cols(m, tiles), P * first : P * first + width
                ],
                in_=o_sb[z][:, cols(m, tiles), :],
            )

        for tm in range(T):
            difference(tm)
        for tm in range(T):
            square(tm)
        for half in range(2):
            inverse_root(half)

        x_interleave(0, 0)
        scales_to_columns()
        x_interleave(0, 1)
        scales_repeat()
        x_interleave(1, 0)
        scales_to_rows()
        x_interleave(1, 1)
        permute_p_codes(0)
        for t in range(T):
            weight(t)
        permute_p_codes(1)
        for tm in range(T):
            g_imaginary(tm)
        g_real()

        x_widen(0, 0)
        x_widen(0, 1)
        q_turn(0, 0)
        q_turn(0, 1)
        q_copy(0, 0)
        q_copy(0, 1)
        x_widen(1, 0)
        q_turn(1, 0)

        g_quantize(1)
        permute_p_planes()
        g_quantize(0)
        x_quantize(0)
        q_quantize(0)

        for c in (1, 0):
            for blk in (0, 1):
                transfer(blk, c)
                keep_transfer(blk, c)
        analysis(0, 0)
        analysis(0, 1)
        x_widen(1, 1)
        for c in (1, 0):
            transfer(2, c)
            keep_transfer(2, c)
        q_turn(1, 1)
        q_copy(1, 0)
        q_copy(1, 1)
        analysis(0, 2)
        for c in (1, 0):
            transfer(3, c)
            keep_transfer(3, c)
        analysis(0, 3)

        filter_block(0, 0)
        filter_block(0, 1)
        f_quantize(0)
        x_quantize(1)
        filter_block(1, 2)
        q_quantize(1)
        filter_block(1, 3)

        analysis(1, 0)
        synthesis(0, 0)
        synthesis(0, 1)
        analysis(1, 1)
        filter_part(2, 0, 0)
        f_quantize(1)
        filter_part(2, 0, 1)
        filter_block(2, 1)
        synthesis(0, 2)
        synthesis(0, 3)
        analysis(1, 2)
        synthesis(1, 0)
        synthesis(1, 1)
        analysis(1, 3)
        filter_part(3, 2, 0)
        f_quantize(2)
        filter_part(3, 2, 1)
        filter_part(4, 3, 0)
        f_quantize(3)
        filter_part(4, 3, 1)
        f_quantize(4)
        synthesis(1, 2)
        synthesis(1, 3)
        for m in range(4):
            synthesis(2, m)
        for z in (3, 4):
            synthesis(z, 0, nc.vector.tensor_copy)
            synthesis(z, 1)
